import numpy as np, ml_dtypes
CORES = [83,85,87,115,117,119]
N = 6
KB, QP = 1, 512
MEM = [2,3,4]
def setup_inputs(rng):
    return {"q": rng.standard_normal((N, 128, QP), dtype=np.float32).astype(ml_dtypes.bfloat16), "k": rng.standard_normal((N, 128, KB * 128), dtype=np.float32).astype(ml_dtypes.bfloat16), "v": rng.standard_normal((N, 128, KB * 128), dtype=np.float32).astype(ml_dtypes.bfloat16)}
def setup_inputs_big(rng):
    d = setup_inputs(rng)
    for k in ("q", "k", "v"): d[k] = (d[k].astype(np.float32) * 1024.0).astype(d[k].dtype)
    return d
def setup_inputs_small(rng):
    d = setup_inputs(rng)
    for k in ("q", "k", "v"): d[k] = (d[k].astype(np.float32) * (1 / 1024.0)).astype(d[k].dtype)
    return d
def setup_inputs_apart(rng):
    d = setup_inputs(rng)
    f = (10.0 ** rng.permutation(np.linspace(-1.5, 1.5, N))).astype(np.float32).reshape(N, 1, 1)
    for k in ("q", "k", "v"): d[k] = (d[k].astype(np.float32) * f).astype(d[k].dtype)
    return d
def reference(q, k, v):
    Q, K, V = q.astype(np.float64), k.astype(np.float64), v.astype(np.float64)
    y = np.zeros((N, 128, QP))
    for r in range(N):
        for j in MEM:
            for b in range(KB):
                S = np.maximum(K[j][:, 128 * b:128 * b + 128].T @ Q[r], 0.0)
                y[r] += V[j][:, 128 * b:128 * b + 128].T @ S
    return {"y": y.astype(ml_dtypes.bfloat16 if q.dtype != np.float64 else np.float64)}

@@ -1,0 +1,136 @@
+from concourse.bass import DstId, RemoteDMATransfer
+from concourse.mybir import AluOpType
+
+NM = 3
+H = 2
+QP = 512
+W = QP // H
+
+SCRATCH = {
+    "qs": ("sbuf", [128, QP], "bfloat16"),
+    "zero": ("sbuf", [128, W], "float32"),
+    "ysb": ("sbuf", [128, QP], "bfloat16"),
+}
+SEMAPHORES = ["ldkv", "ldq", "sent", "zr"]
+for _m in range(NM):
+    SCRATCH["kv%d" % _m] = ("sbuf", [128, 256], "bfloat16")
+    SCRATCH["sb%d" % _m] = ("sbuf", [128, QP], "bfloat16")
+    SEMAPHORES.append("arr%d" % _m)
+    for _h in range(H):
+        SCRATCH["ps%d_%d" % (_m, _h)] = ("psum", [128, 512], "float32")
+        SEMAPHORES.append("m1_%d_%d" % (_m, _h))
+        SEMAPHORES.append("rl_%d_%d" % (_m, _h))
+for _h in range(H):
+    SCRATCH["po%d" % _h] = ("psum", [128, 512], "float32")
+    SEMAPHORES += ["m2_%d" % _h, "cp%d" % _h, "st%d" % _h]
+
+
+def _bits(mask):
+    return bin(mask).count("1")
+
+
+def _plan(m, T, topo):
+    src = T.cores[T.tables["MEM"][m]]
+    far = [c for c in T.cores if c != src and topo.chip(c) != topo.chip(src)]
+    near = [c for c in T.cores if c != src and topo.chip(c) == topo.chip(src)]
+    rot = lambda l: l[m % len(l):] + l[:m % len(l)] if l else l
+    return src, rot(far), rot(near)
+
+
+def _send(g, T, topo, src, dsts, tile, mask, sem):
+    ids = []
+    for d in dsts:
+        assert topo.may_write(src, d)
+        rid, pid, _ = topo.addr(d)
+        ids.append(DstId(rid=rid, pnc=pid))
+    g.remote_dma_fused([RemoteDMATransfer(dst_ids=ids, dma_engine_mask=mask, remote_sem=sem,
+                                          srcs=[tile[:]], dsts=[tile[:] for _ in dsts], alu_op=0)],
+                       local_sem=T.sem.sent)
+    return _bits(mask)
+
+
+def rank_program(g, core, T, topo):
+    rank = T.rank_of(core)
+    if rank is None:
+        return
+    mem = T.tables["MEM"]
+    kv = [T["kv%d" % m] for m in range(NM)]
+    sb = [T["sb%d" % m] for m in range(NM)]
+    mine = mem.index(rank) if rank in mem else None
+
+    if mine is not None:
+        g.sync.dma_start(kv[mine][:, 0:128], T.k[:]).then_inc(T.sem.ldkv, 16)
+        g.scalar.dma_start(kv[mine][:, 128:256], T.v[:]).then_inc(T.sem.ldkv, 16)
+    g.sync.dma_start(T.qs[:], T.q[:]).then_inc(T.sem.ldq, 16)
+    g.vector.memset(T.zero[:], 0.0).then_inc(T.sem.zr, 1)
+
+    need = {}
+    when = {}
+    for m in range(NM):
+        src, far, near = _plan(m, T, topo)
+        if src == core:
+            when[m] = (0, 0)
+            continue
+        out = 0
+        for d in far:
+            out |= topo.mask(src, d)
+        if core in far:
+            need[m] = _bits(out)
+            when[m] = (2, far.index(core))
+        else:
+            need[m] = _bits(topo.mask(src, core) & ~out)
+            when[m] = (1, near.index(core))
+    order = sorted(range(NM), key=lambda m: when[m])
+
+    if mine is not None:
+        src, far, near = _plan(mine, T, topo)
+        out = 0
+        for d in far:
+            out |= topo.mask(src, d)
+        g.wait_ge(T.sem.ldkv, 32)
+        n = _send(g, T, topo, src, far, kv[mine], out, T.sem["arr%d" % mine])
+        inn = topo.mask(src, near[0]) & ~out
+        n += _send(g, T, topo, src, near, kv[mine], inn, T.sem["arr%d" % mine])
+        g.wait_ge(T.sem.sent, n)
+
+    te = g.tensor
+
+    def mm1(m):
+        if m == mine:
+            te.wait_ge(T.sem.ldkv, 32)
+        else:
+            te.wait_ge(T.sem["arr%d" % m], need[m])
+        for h in range(H):
+            te.matmul(T["ps%d_%d" % (m, h)][:, 0:W], kv[m][:, 0:128], T.qs[:, h * W:(h + 1) * W],
+                      True, True).then_inc(T.sem["m1_%d_%d" % (m, h)], 1)
+
+    def mm2(i):
+        m = order[i]
+        for h in range(H):
+            te.wait_ge(T.sem["rl_%d_%d" % (m, h)], 1)
+            te.matmul(T["po%d" % h][:, 0:W], kv[m][:, 128:256], sb[m][:, h * W:(h + 1) * W],
+                      i == 0, i == NM - 1).then_inc(T.sem["m2_%d" % h], 1)
+
+    te.wait_ge(T.sem.ldq, 16)
+    mm1(order[0])
+    for i in range(1, NM):
+        mm1(order[i])
+        mm2(i - 1)
+    mm2(NM - 1)
+
+    ve = g.vector
+    ve.wait_ge(T.sem.zr, 1)
+    for m in order:
+        for h in range(H):
+            ve.wait_ge(T.sem["m1_%d_%d" % (m, h)], 1)
+            ve.tensor_tensor(sb[m][:, h * W:(h + 1) * W], T["ps%d_%d" % (m, h)][:, 0:W], T.zero[:],
+                             AluOpType.max).then_inc(T.sem["rl_%d_%d" % (m, h)], 1)
+    for h in range(H):
+        ve.wait_ge(T.sem["m2_%d" % h], NM)
+        ve.tensor_copy(T.ysb[:, h * W:(h + 1) * W], T["po%d" % h][:, 0:W]).then_inc(T.sem["cp%d" % h], 1)
+
+    for h in range(H):
+        qu = g.sync if h % 2 == 0 else g.scalar
+        qu.wait_ge(T.sem["cp%d" % h], 1)
+        qu.dma_start(T.y[:, h * W:(h + 1) * W], T.ysb[:, h * W:(h + 1) * W]).then_inc(T.sem["st%d" % h], 16)
+        qu.wait_ge(T.sem["st%d" % h], 16)

@@ -5,24 +5,27 @@ NM = 3
 H = 2
 QP = 512
 W = QP // H
+OB = [(0, 128, 0), (128, 256, 0), (256, 384, 1), (384, 512, 1)]
 
 SCRATCH = {
     "qs": ("sbuf", [128, QP], "bfloat16"),
     "zero": ("sbuf", [128, W], "float32"),
     "ysb": ("sbuf", [128, QP], "bfloat16"),
 }
-SEMAPHORES = ["ldkv", "ldq", "sent", "zr"]
+SEMAPHORES = ["ldk", "ldv", "ldq", "sent", "zr", "st0", "st1"]
 for _m in range(NM):
     SCRATCH["kv%d" % _m] = ("sbuf", [128, 256], "bfloat16")
     SCRATCH["sb%d" % _m] = ("sbuf", [128, QP], "bfloat16")
-    SEMAPHORES.append("arr%d" % _m)
+    SEMAPHORES += ["ak%d" % _m, "av%d" % _m]
     for _h in range(H):
-        SCRATCH["ps%d_%d" % (_m, _h)] = ("psum", [128, 512], "float32")
         SEMAPHORES.append("m1_%d_%d" % (_m, _h))
         SEMAPHORES.append("rl_%d_%d" % (_m, _h))
-for _h in range(H):
-    SCRATCH["po%d" % _h] = ("psum", [128, 512], "float32")
-    SEMAPHORES += ["m2_%d" % _h, "cp%d" % _h, "st%d" % _h]
+for _s in range(2):
+    for _h in range(H):
+        SCRATCH["ps%d_%d" % (_s, _h)] = ("psum", [128, 512], "float32")
+for _b in range(len(OB)):
+    SCRATCH["po%d" % _b] = ("psum", [128, 512], "float32")
+    SEMAPHORES += ["m2_%d" % _b, "cp%d" % _b]
 
 
 def _bits(mask):
@@ -30,23 +33,29 @@ def _bits(mask):
 
 
 def _plan(m, T, topo):
-    src = T.cores[T.tables["MEM"][m]]
-    far = [c for c in T.cores if c != src and topo.chip(c) != topo.chip(src)]
-    near = [c for c in T.cores if c != src and topo.chip(c) == topo.chip(src)]
-    rot = lambda l: l[m % len(l):] + l[:m % len(l)] if l else l
-    return src, rot(far), rot(near)
+    mem = T.tables["MEM"]
+    owners = [T.cores[r] for r in mem]
+    src = owners[m]
+    first = lambda l: [c for c in l if c not in owners] + [c for c in l if c in owners]
+    far = first([c for c in T.cores if c != src and topo.chip(c) != topo.chip(src)])
+    near = first([c for c in T.cores if c != src and topo.chip(c) == topo.chip(src)])
+    place = [o for o in owners if topo.chip(o) == topo.chip(src)].index(src)
+    far = far[place % len(far):] + far[:place % len(far)]
+    out = 0
+    for d in far:
+        out |= topo.mask(src, d)
+    inn = topo.mask(src, near[0]) & ~out
+    return src, far, near, out, inn
 
 
-def _send(g, T, topo, src, dsts, tile, mask, sem):
+def _tr(T, topo, src, dsts, ap, mask, sem):
     ids = []
     for d in dsts:
         assert topo.may_write(src, d)
         rid, pid, _ = topo.addr(d)
         ids.append(DstId(rid=rid, pnc=pid))
-    g.remote_dma_fused([RemoteDMATransfer(dst_ids=ids, dma_engine_mask=mask, remote_sem=sem,
-                                          srcs=[tile[:]], dsts=[tile[:] for _ in dsts], alu_op=0)],
-                       local_sem=T.sem.sent)
-    return _bits(mask)
+    return RemoteDMATransfer(dst_ids=ids, dma_engine_mask=mask, remote_sem=sem,
+                             srcs=[ap], dsts=[ap for _ in dsts], alu_op=0)
 
 
 def rank_program(g, core, T, topo):
@@ -59,78 +68,94 @@ def rank_program(g, core, T, topo):
     mine = mem.index(rank) if rank in mem else None
 
     if mine is not None:
-        g.sync.dma_start(kv[mine][:, 0:128], T.k[:]).then_inc(T.sem.ldkv, 16)
-        g.scalar.dma_start(kv[mine][:, 128:256], T.v[:]).then_inc(T.sem.ldkv, 16)
+        g.sync.dma_start(kv[mine][:, 0:128], T.k[:]).then_inc(T.sem.ldk, 16)
+        g.scalar.dma_start(kv[mine][:, 128:256], T.v[:]).then_inc(T.sem.ldv, 16)
     g.sync.dma_start(T.qs[:], T.q[:]).then_inc(T.sem.ldq, 16)
     g.vector.memset(T.zero[:], 0.0).then_inc(T.sem.zr, 1)
 
     need = {}
-    when = {}
+    kwhen = {}
+    vwhen = {}
     for m in range(NM):
-        src, far, near = _plan(m, T, topo)
+        src, far, near, out, inn = _plan(m, T, topo)
         if src == core:
-            when[m] = (0, 0)
-            continue
-        out = 0
-        for d in far:
-            out |= topo.mask(src, d)
-        if core in far:
+            kwhen[m] = (-1, 0)
+            vwhen[m] = (-1, 0)
+        elif core in far:
             need[m] = _bits(out)
-            when[m] = (2, far.index(core))
+            kwhen[m] = (far.index(core), 0)
+            vwhen[m] = (1, far.index(core))
         else:
-            need[m] = _bits(topo.mask(src, core) & ~out)
-            when[m] = (1, near.index(core))
-    order = sorted(range(NM), key=lambda m: when[m])
+            need[m] = _bits(inn)
+            kwhen[m] = (near.index(core), 1)
+            vwhen[m] = (0, near.index(core))
+    korder = sorted(range(NM), key=lambda m: kwhen[m])
+    vorder = sorted(range(NM), key=lambda m: vwhen[m])
+    slot = {m: i % 2 for i, m in enumerate(korder)}
 
     if mine is not None:
-        src, far, near = _plan(mine, T, topo)
-        out = 0
-        for d in far:
-            out |= topo.mask(src, d)
-        g.wait_ge(T.sem.ldkv, 32)
-        n = _send(g, T, topo, src, far, kv[mine], out, T.sem["arr%d" % mine])
-        inn = topo.mask(src, near[0]) & ~out
-        n += _send(g, T, topo, src, near, kv[mine], inn, T.sem["arr%d" % mine])
-        g.wait_ge(T.sem.sent, n)
+        src, far, near, out, inn = _plan(mine, T, topo)
+        ka, va = kv[mine][:, 0:128], kv[mine][:, 128:256]
+        sk, sv = T.sem["ak%d" % mine], T.sem["av%d" % mine]
+        g.wait_ge(T.sem.ldk, 16)
+        g.remote_dma_fused([_tr(T, topo, src, far, ka, out, sk)], local_sem=T.sem.sent)
+        g.remote_dma_fused([_tr(T, topo, src, near, ka, inn, sk)], local_sem=T.sem.sent)
+        g.wait_ge(T.sem.ldv, 16)
+        g.remote_dma_fused([_tr(T, topo, src, far, va, out, sv), _tr(T, topo, src, near, va, inn, sv)],
+                           local_sem=T.sem.sent)
+        g.wait_ge(T.sem.sent, 2 * (_bits(out) + _bits(inn)))
 
     te = g.tensor
 
-    def mm1(m):
+    def mm1(i):
+        m = korder[i]
         if m == mine:
-            te.wait_ge(T.sem.ldkv, 32)
+            te.wait_ge(T.sem.ldk, 16)
         else:
-            te.wait_ge(T.sem["arr%d" % m], need[m])
+            te.wait_ge(T.sem["ak%d" % m], need[m])
         for h in range(H):
-            te.matmul(T["ps%d_%d" % (m, h)][:, 0:W], kv[m][:, 0:128], T.qs[:, h * W:(h + 1) * W],
+            if i >= 2:
+                te.wait_ge(T.sem["rl_%d_%d" % (korder[i - 2], h)], 1)
+            te.matmul(T["ps%d_%d" % (slot[m], h)][:, 0:W], kv[m][:, 0:128], T.qs[:, h * W:(h + 1) * W],
                       True, True).then_inc(T.sem["m1_%d_%d" % (m, h)], 1)
 
     def mm2(i):
-        m = order[i]
-        for h in range(H):
+        m = vorder[i]
+        if m == mine:
+            te.wait_ge(T.sem.ldv, 16)
+        else:
+            te.wait_ge(T.sem["av%d" % m], need[m])
+        for b, (c0, c1, h) in enumerate(OB):
             te.wait_ge(T.sem["rl_%d_%d" % (m, h)], 1)
-            te.matmul(T["po%d" % h][:, 0:W], kv[m][:, 128:256], sb[m][:, h * W:(h + 1) * W],
-                      i == 0, i == NM - 1).then_inc(T.sem["m2_%d" % h], 1)
+            te.matmul(T["po%d" % b][:, 0:c1 - c0], kv[m][:, 128:256], sb[m][:, c0:c1],
+                      i == 0, i == NM - 1).then_inc(T.sem["m2_%d" % b], 1)
 
     te.wait_ge(T.sem.ldq, 16)
-    mm1(order[0])
-    for i in range(1, NM):
-        mm1(order[i])
-        mm2(i - 1)
-    mm2(NM - 1)
+    done2 = 0
+    for i, m in enumerate(korder):
+        mm1(i)
+        if m == mine:
+            mm2(0)
+            done2 = 1
+    for i in range(done2, NM):
+        mm2(i)
 
     ve = g.vector
     ve.wait_ge(T.sem.zr, 1)
-    for m in order:
+    for m in korder:
         for h in range(H):
             ve.wait_ge(T.sem["m1_%d_%d" % (m, h)], 1)
-            ve.tensor_tensor(sb[m][:, h * W:(h + 1) * W], T["ps%d_%d" % (m, h)][:, 0:W], T.zero[:],
+            ve.tensor_tensor(sb[m][:, h * W:(h + 1) * W], T["ps%d_%d" % (slot[m], h)][:, 0:W], T.zero[:],
                              AluOpType.max).then_inc(T.sem["rl_%d_%d" % (m, h)], 1)
-    for h in range(H):
-        ve.wait_ge(T.sem["m2_%d" % h], NM)
-        ve.tensor_copy(T.ysb[:, h * W:(h + 1) * W], T["po%d" % h][:, 0:W]).then_inc(T.sem["cp%d" % h], 1)
+    for b, (c0, c1, _) in enumerate(OB):
+        ve.wait_ge(T.sem["m2_%d" % b], NM)
+        ve.tensor_copy(T.ysb[:, c0:c1], T["po%d" % b][:, 0:c1 - c0]).then_inc(T.sem["cp%d" % b], 1)
 
-    for h in range(H):
-        qu = g.sync if h % 2 == 0 else g.scalar
-        qu.wait_ge(T.sem["cp%d" % h], 1)
-        qu.dma_start(T.y[:, h * W:(h + 1) * W], T.ysb[:, h * W:(h + 1) * W]).then_inc(T.sem["st%d" % h], 16)
-        qu.wait_ge(T.sem["st%d" % h], 16)
+    g.sync.wait_ge(T.sem.cp0, 1)
+    g.sync.wait_ge(T.sem.cp1, 1)
+    g.sync.dma_start(T.y[:, 0:W], T.ysb[:, 0:W]).then_inc(T.sem.st0, 16)
+    g.scalar.wait_ge(T.sem.cp2, 1)
+    g.scalar.wait_ge(T.sem.cp3, 1)
+    g.scalar.dma_start(T.y[:, W:QP], T.ysb[:, W:QP]).then_inc(T.sem.st1, 16)
+    g.sync.wait_ge(T.sem.st0, 16)
+    g.scalar.wait_ge(T.sem.st1, 16)

from concourse.bass import DstId, RemoteDMATransfer
from concourse.mybir import AluOpType

NM = 3
H = 2
QP = 512
W = QP // H
OB = [(0, 128, 0), (128, 256, 0), (256, 384, 1), (384, 512, 1)]

SCRATCH = {
    "qs": ("sbuf", [128, QP], "bfloat16"),
    "zero": ("sbuf", [128, W], "float32"),
    "ysb": ("sbuf", [128, QP], "bfloat16"),
}
SEMAPHORES = ["ldk", "ldv", "ldq", "sent", "zr", "st0", "st1"]
for _m in range(NM):
    SCRATCH["kv%d" % _m] = ("sbuf", [128, 256], "bfloat16")
    SCRATCH["sb%d" % _m] = ("sbuf", [128, QP], "bfloat16")
    SEMAPHORES += ["ak%d" % _m, "av%d" % _m]
    for _h in range(H):
        SEMAPHORES.append("m1_%d_%d" % (_m, _h))
        SEMAPHORES.append("rl_%d_%d" % (_m, _h))
for _s in range(2):
    for _h in range(H):
        SCRATCH["ps%d_%d" % (_s, _h)] = ("psum", [128, 512], "float32")
for _b in range(len(OB)):
    SCRATCH["po%d" % _b] = ("psum", [128, 512], "float32")
    SEMAPHORES += ["m2_%d" % _b, "cp%d" % _b]


def _bits(mask):
    return bin(mask).count("1")


def _plan(m, T, topo):
    mem = T.tables["MEM"]
    owners = [T.cores[r] for r in mem]
    src = owners[m]
    first = lambda l: [c for c in l if c not in owners] + [c for c in l if c in owners]
    far = first([c for c in T.cores if c != src and topo.chip(c) != topo.chip(src)])
    near = first([c for c in T.cores if c != src and topo.chip(c) == topo.chip(src)])
    place = [o for o in owners if topo.chip(o) == topo.chip(src)].index(src)
    far = far[place % len(far):] + far[:place % len(far)]
    out = 0
    for d in far:
        out |= topo.mask(src, d)
    inn = topo.mask(src, near[0]) & ~out
    return src, far, near, out, inn


def _tr(T, topo, src, dsts, ap, mask, sem):
    ids = []
    for d in dsts:
        assert topo.may_write(src, d)
        rid, pid, _ = topo.addr(d)
        ids.append(DstId(rid=rid, pnc=pid))
    return RemoteDMATransfer(dst_ids=ids, dma_engine_mask=mask, remote_sem=sem,
                             srcs=[ap], dsts=[ap for _ in dsts], alu_op=0)


def rank_program(g, core, T, topo):
    rank = T.rank_of(core)
    if rank is None:
        return
    mem = T.tables["MEM"]
    kv = [T["kv%d" % m] for m in range(NM)]
    sb = [T["sb%d" % m] for m in range(NM)]
    mine = mem.index(rank) if rank in mem else None

    if mine is not None:
        g.sync.dma_start(kv[mine][:, 0:128], T.k[:]).then_inc(T.sem.ldk, 16)
        g.scalar.dma_start(kv[mine][:, 128:256], T.v[:]).then_inc(T.sem.ldv, 16)
    g.sync.dma_start(T.qs[:], T.q[:]).then_inc(T.sem.ldq, 16)
    g.vector.memset(T.zero[:], 0.0).then_inc(T.sem.zr, 1)

    need = {}
    kwhen = {}
    vwhen = {}
    for m in range(NM):
        src, far, near, out, inn = _plan(m, T, topo)
        if src == core:
            kwhen[m] = (-1, 0)
            vwhen[m] = (-1, 0)
        elif core in far:
            need[m] = _bits(out)
            kwhen[m] = (far.index(core), 0)
            vwhen[m] = (1, far.index(core))
        else:
            need[m] = _bits(inn)
            kwhen[m] = (near.index(core), 1)
            vwhen[m] = (0, near.index(core))
    korder = sorted(range(NM), key=lambda m: kwhen[m])
    vorder = sorted(range(NM), key=lambda m: vwhen[m])
    slot = {m: i % 2 for i, m in enumerate(korder)}

    if mine is not None:
        src, far, near, out, inn = _plan(mine, T, topo)
        ka, va = kv[mine][:, 0:128], kv[mine][:, 128:256]
        sk, sv = T.sem["ak%d" % mine], T.sem["av%d" % mine]
        g.wait_ge(T.sem.ldk, 16)
        g.remote_dma_fused([_tr(T, topo, src, far, ka, out, sk)], local_sem=T.sem.sent)
        g.remote_dma_fused([_tr(T, topo, src, near, ka, inn, sk)], local_sem=T.sem.sent)
        g.wait_ge(T.sem.ldv, 16)
        g.remote_dma_fused([_tr(T, topo, src, far, va, out, sv), _tr(T, topo, src, near, va, inn, sv)],
                           local_sem=T.sem.sent)
        g.wait_ge(T.sem.sent, 2 * (_bits(out) + _bits(inn)))

    te = g.tensor

    def mm1(i):
        m = korder[i]
        if m == mine:
            te.wait_ge(T.sem.ldk, 16)
        else:
            te.wait_ge(T.sem["ak%d" % m], need[m])
        for h in range(H):
            if i >= 2:
                te.wait_ge(T.sem["rl_%d_%d" % (korder[i - 2], h)], 1)
            te.matmul(T["ps%d_%d" % (slot[m], h)][:, 0:W], kv[m][:, 0:128], T.qs[:, h * W:(h + 1) * W],
                      True, True).then_inc(T.sem["m1_%d_%d" % (m, h)], 1)

    def mm2(i):
        m = vorder[i]
        if m == mine:
            te.wait_ge(T.sem.ldv, 16)
        else:
            te.wait_ge(T.sem["av%d" % m], need[m])
        for b, (c0, c1, h) in enumerate(OB):
            te.wait_ge(T.sem["rl_%d_%d" % (m, h)], 1)
            te.matmul(T["po%d" % b][:, 0:c1 - c0], kv[m][:, 128:256], sb[m][:, c0:c1],
                      i == 0, i == NM - 1).then_inc(T.sem["m2_%d" % b], 1)

    te.wait_ge(T.sem.ldq, 16)
    done2 = 0
    for i, m in enumerate(korder):
        mm1(i)
        if m == mine:
            mm2(0)
            done2 = 1
    for i in range(done2, NM):
        mm2(i)

    ve = g.vector
    ve.wait_ge(T.sem.zr, 1)
    for m in korder:
        for h in range(H):
            ve.wait_ge(T.sem["m1_%d_%d" % (m, h)], 1)
            ve.tensor_tensor(sb[m][:, h * W:(h + 1) * W], T["ps%d_%d" % (slot[m], h)][:, 0:W], T.zero[:],
                             AluOpType.max).then_inc(T.sem["rl_%d_%d" % (m, h)], 1)
    for b, (c0, c1, _) in enumerate(OB):
        ve.wait_ge(T.sem["m2_%d" % b], NM)
        ve.tensor_copy(T.ysb[:, c0:c1], T["po%d" % b][:, 0:c1 - c0]).then_inc(T.sem["cp%d" % b], 1)

    g.sync.wait_ge(T.sem.cp0, 1)
    g.sync.wait_ge(T.sem.cp1, 1)
    g.sync.dma_start(T.y[:, 0:W], T.ysb[:, 0:W]).then_inc(T.sem.st0, 16)
    g.scalar.wait_ge(T.sem.cp2, 1)
    g.scalar.wait_ge(T.sem.cp3, 1)
    g.scalar.dma_start(T.y[:, W:QP], T.ysb[:, W:QP]).then_inc(T.sem.st1, 16)
    g.sync.wait_ge(T.sem.st0, 16)
    g.scalar.wait_ge(T.sem.st1, 16)
